import numpy as np
import ml_dtypes


def mxq(x, axis, fmt="e4m3"):
    dtype, down = {"e4m3": (ml_dtypes.float8_e4m3fn, 7), "e5m2": (ml_dtypes.float8_e5m2, 14)}[fmt]
    v = np.moveaxis(np.asarray(x, np.float32).astype(ml_dtypes.bfloat16).astype(np.float64), axis, -1)
    blocks = v.reshape(v.shape[:-1] + (-1, 32))
    amax = np.abs(blocks).max(-1, keepdims=True)
    byte = np.maximum(np.where(amax > 0, np.frexp(amax)[1] - 1 + 127, 0) - down, 1)
    scale = np.exp2(byte - 127.0)
    codes = (blocks / scale).astype(np.float32).astype(dtype).astype(np.float64)
    return np.moveaxis((codes * scale).reshape(v.shape), -1, axis)


WIDE = False


def mx_kscale(k):
    if not WIDE:
        return np.ones(k)
    levels = np.array([10, -10, 5, -5, 0])
    if k % 512:
        return np.exp2(np.random.permutation(np.resize(levels, k // 32))).repeat(32)
    a = np.empty((k // 512, 16))
    for p in range(k // 512):
        a[p, :8] = np.random.permutation(np.resize(levels, 8))
        for g in range(8):
            far = levels[np.abs(levels - a[p, g]) >= 10]
            a[p, g + 8] = far[np.random.randint(len(far))]
    return np.exp2(a.ravel()).repeat(32)


def f64(x):
    return np.asarray(x).astype(np.float64)


def striped(idx):
    return np.tile(idx.reshape(-1, 16).T, (8, 1)).astype(np.uint16)


def unstriped(offs):
    return offs[:16].T.reshape(-1).astype(np.int64)


K, T, E, C, N = 512, 1024, 24, 128, 128
TOP = 3


def by_expert(wq, xq):
    return np.concatenate([wq[e].T @ xq[:, e * C:(e + 1) * C] for e in range(E)], axis=1)


def setup_inputs():
    n = np.random.standard_normal
    s = mx_kscale(K)[:, None]
    deal = np.repeat(np.arange(E), C).reshape(TOP, T)[:, np.random.permutation(T)]
    deal = np.take_along_axis(deal, np.argsort(np.random.rand(TOP, T), axis=0), axis=0)
    for _ in range(8):
        s_, t_ = np.random.permutation(T).reshape(2, -1); r = np.random.randint(TOP, size=T // 2); x, y = deal[r, s_].copy(), deal[r, t_].copy()
        ok = ~((deal[:, s_] == y).any(0) | (deal[:, t_] == x).any(0)); deal[r[ok], s_[ok]] = y[ok]; deal[r[ok], t_[ok]] = x[ok]
    order = np.lexsort((np.random.rand(TOP * T), deal.reshape(-1)))
    slot_token = order % T; pos = np.empty(TOP * T, np.int64); pos[order] = np.arange(TOP * T); pos = pos.reshape(TOP, T)
    g = np.random.uniform(0.5, 1.5, (TOP, T)); g = g / g.sum(0)
    return {
        "xT": (n((K, T)) * s).astype(np.float32),
        "w": (n((E + 1, K, N)) / np.sqrt(K) / s[None]).astype(np.float32),
        "b": (0.3 * n((N, E + 1))).astype(np.float32),
        "gate": np.stack([np.tile(r, (N, 1)) for r in g]).astype(np.float32),
        "offs": striped(slot_token),
        "pos1": striped(pos[0]),
        "pos2": striped(pos[1]),
        "pos3": striped(pos[2]),
    }


def reference(xT, w, b, gate, offs, pos1, pos2, pos3):
    idx = unstriped(offs)
    wq = mxq(f64(w), 1, "e4m3")
    xs = mxq(f64(xT), 0, "e4m3")
    ys = (wq[E].T @ xs) + f64(b)[:, E:]
    xq = mxq(f64(xT)[:, idx], 0, "e4m3")
    y = by_expert(wq, xq)
    y = y + np.repeat(f64(b)[:, :E], C, axis=1)
    return ys + sum(f64(gate[r]) * y[:, unstriped(p)] for r, p in enumerate((pos1, pos2, pos3)))

@@ -1,0 +1,256 @@
+from contextlib import ExitStack
+
+import concourse.mybir as mybir
+from concourse.masks import make_identity
+
+K, T, E, C, N = 512, 1024, 24, 128, 128
+TOP = 3
+SLOTS = E * C
+FLOPS = 2 * K * N * (SLOTS + T)
+
+F32 = mybir.dt.float32
+BF16 = mybir.dt.bfloat16
+I32 = mybir.dt.int32
+U32 = mybir.dt.uint32
+U16 = mybir.dt.uint16
+U8 = mybir.dt.uint8
+FP8X4 = mybir.dt.float8_e4m3fn_x4
+IDENTITY = mybir.ActivationFunctionType.Identity
+COPY = mybir.ActivationFunctionType.Copy
+ADD = mybir.AluOpType.add
+MULT = mybir.AluOpType.mult
+
+P = 128
+PACK = 4
+GROUP = 4
+CHUNK = GROUP * C
+CHUNKS = E // GROUP
+HALF = T // 2
+BLOCKS = HALF // P
+LIST_COLS = CHUNK // 16
+
+
+def tile_moe_shr_lin_bias_kernel(tc, xT, w, b, gate, offs, pos1, pos2, pos3, out):
+    nc = tc.nc
+    with ExitStack() as ctx:
+        lists = ctx.enter_context(tc.tile_pool(name="lists", bufs=1))
+        keep = ctx.enter_context(tc.tile_pool(name="keep", bufs=1))
+        shared = ctx.enter_context(tc.tile_pool(name="shared", bufs=1))
+        psum = ctx.enter_context(tc.psum_pool(name="psum", bufs=1))
+
+        def tiles(pool, name, count, shape, dtype):
+            return [pool.tile(shape, dtype, name="%s%d" % (name, i), align_bytes=64) for i in range(count)]
+
+        offs_sb = lists.tile([P, SLOTS // 16], U16, name="offs_sb")
+        pos_sb = [lists.tile([P, T // 16], U16, name="pos_sb%d" % r) for r in range(TOP)]
+
+        x_raw = tiles(keep, "x_raw", 4, [P, 2, HALF], F32)
+        room = 4 * GROUP * K
+
+        def placed(name, shape, dtype, offset):
+            return shared.tile(shape, dtype, name=name, align_bytes=64, offset=offset)
+
+        w_raw = [None] + [placed("w_raw%d" % c, [P, GROUP * K], F32, c * room) for c in range(1, CHUNKS)]
+        w0_raw = [placed("w0_raw%d" % i, [P, 2 * K], F32, i * room // 2) for i in range(2)]
+        ws_raw = keep.tile([P, K], F32, name="ws_raw", align_bytes=64)
+        pairs = keep.tile([P, 2 * T], U32, name="pairs", align_bytes=64)
+        gathered = tiles(keep, "gathered", 2, [P, 2 * CHUNK], U32)
+        gathered = gathered + [placed("gathered%d" % c, [P, 2 * CHUNK], U32, (c - 2) * room) for c in range(2, CHUNKS)]
+        x_bf = tiles(keep, "x_bf", 1, [P, PACK * CHUNK], BF16)
+        x_bf = x_bf + [placed("x_bf%d" % c, [P, PACK * CHUNK], BF16, (c - 1) * room + room // 2) for c in range(1, CHUNKS)]
+        xs_codes = [placed("xs_codes%d" % h, [P, HALF], U32, (CHUNKS - 1) * room + h * room // 4) for h in range(2)]
+        xs_scales = tiles(keep, "xs_scales", 2, [P, HALF], U8)
+        x_codes = tiles(keep, "x_codes", 2, [P, CHUNK], U32)
+        last_scales = keep.tile([P, CHUNK], U8, name="last_scales", align_bytes=64)
+        w_bf = tiles(keep, "w_bf", 3, [P, GROUP * K], BF16)
+        w_codes = tiles(keep, "w_codes", 2, [P, GROUP * N], U32)
+        w_scales = tiles(keep, "w_scales", 2, [P, GROUP * N], U8)
+        ws_bf = keep.tile([P, K], BF16, name="ws_bf", align_bytes=64)
+        ws_codes = keep.tile([P, N], U32, name="ws_codes", align_bytes=64)
+        ws_scales = keep.tile([P, N], U8, name="ws_scales", align_bytes=64)
+        xs_bf = tiles(keep, "xs_bf", 2, [P, PACK * HALF], BF16)
+        bias = keep.tile([P, E + 1], F32, name="bias", align_bytes=64)
+        ident = keep.tile([P, P], F32, name="ident", align_bytes=64)
+        gate_rows = keep.tile([P, P], F32, name="gate_rows", align_bytes=64)
+        gate_cols = keep.tile([P, P], F32, name="gate_cols", align_bytes=64)
+        gate_last = keep.tile([P, HALF], F32, name="gate_last", align_bytes=64)
+        y = keep.tile([P, SLOTS], F32, name="y", align_bytes=64)
+        ys_t = tiles(keep, "ys_t", 2, [P, HALF], F32)
+        picked = tiles(keep, "picked", 6, [P, HALF], F32)
+        scaled = tiles(keep, "scaled", 5, [P, HALF], F32)
+        result = tiles(keep, "result", 2, [P, HALF], F32)
+
+        banks = [psum.tile([P, 512], F32, name="bank%d" % i) for i in range(6)]
+        sum_bank = [psum.tile([P, 512], F32, name="sum_bank%d" % i) for i in range(2)]
+
+        x_rows = xT.rearrange("(p j) t -> p j t", j=PACK)
+        w_rows = w.rearrange("e (p j) n -> p e (j n)", j=PACK)
+
+        def load_x(u, h):
+            nc.sync.dma_start(out=x_raw[2 * u + h][:], in_=x_rows[:, 2 * u : 2 * u + 2, h * HALF : (h + 1) * HALF])
+
+        def load_w(dst, e0, count):
+            nc.sync.dma_start(out=dst[:].rearrange("p (e f) -> p e f", e=count), in_=w_rows[:, e0 : e0 + count, :])
+
+        load_x(0, 0)
+        load_x(0, 1)
+        nc.sync.dma_start(offs_sb[:], offs)
+        load_x(1, 0)
+        load_x(1, 1)
+        load_w(w0_raw[0], 0, 2)
+        load_w(w0_raw[1], 2, 2)
+        nc.sync.dma_start(out=bias[:], in_=b)
+        load_w(w_raw[1], GROUP, GROUP)
+        load_w(ws_raw, E, 1)
+        for c in range(2, CHUNKS):
+            load_w(w_raw[c], GROUP * c, GROUP)
+
+        make_identity(nc, ident[:])
+        nc.scalar.activation(out=gate_rows[:], in_=ident[:], func=IDENTITY, scale=0.0)
+        for r in range(TOP):
+            nc.sync.dma_start(
+                out=gate_rows[32 * r : 32 * r + T // P, :], in_=gate[r, 0, :].rearrange("(c p) -> c p", p=P)
+            )
+        nc.sync.dma_start(out=gate_last[:], in_=gate[TOP - 1, :, HALF:])
+        for r, pos in enumerate((pos1, pos2, pos3)):
+            nc.sync.dma_start(pos_sb[r][:], pos)
+
+        def cast_x(engine_copy, u, h):
+            dst = pairs[:, u * T + h * HALF : u * T + (h + 1) * HALF].bitcast(BF16)
+            engine_copy(
+                out=dst.rearrange("p (c i j) -> p c j i", i=4, j=2),
+                in_=x_raw[2 * u + h][:].rearrange("p j (c i) -> p c j i", i=4),
+            )
+
+        def cast_w(dst, src, count):
+            nc.scalar.copy(
+                out=dst.rearrange("p (e c i j) -> p e c j i", e=count, i=4, j=PACK),
+                in_=src.rearrange("p (e j c i) -> p e c j i", e=count, i=4, j=PACK),
+            )
+
+        def cast_w_chunk(c):
+            if c == 0:
+                for s in range(2):
+                    cast_w(w_bf[0][:, s * 2 * K : (s + 1) * 2 * K], w0_raw[s][:], 2)
+            else:
+                cast_w(w_bf[c % 3][:], w_raw[c][:], GROUP)
+
+        def gather(u, c):
+            nc.vector.tensor_copy(
+                out=gathered[c][:, u * CHUNK : (u + 1) * CHUNK],
+                in_=pairs[:, u * T : (u + 1) * T].indirect(offs_sb[:, c * LIST_COLS : (c + 1) * LIST_COLS]),
+            )
+
+        def weave(c):
+            nc.vector.tensor_copy(
+                out=x_bf[c][:].bitcast(I32).rearrange("p (s u) -> p s u", u=2),
+                in_=gathered[c][:].bitcast(I32).rearrange("p (u s) -> p s u", u=2),
+            )
+
+        def weave_shared(h):
+            nc.scalar.copy(
+                out=xs_bf[h][:].bitcast(U32).rearrange("p (s u) -> p s u", u=2),
+                in_=pairs[:].rearrange("p (u s) -> p s u", u=2)[:, h * HALF : (h + 1) * HALF, :],
+            )
+
+        def quantize(codes, scales, src):
+            nc.vector.quantize_mx(out=codes[:].bitcast(FP8X4), scales=scales, in_=src[:])
+
+        def x_scales(c):
+            return last_scales[:] if c == CHUNKS - 1 else w_scales[c % 2][4:, :]
+
+        def mx(dst, l_codes, l_scales, r_codes, r_scales):
+            nc.tensor.matmul_mx(
+                out=dst, lhsT=l_codes.bitcast(FP8X4), lhsT_scale=l_scales,
+                rhs=r_codes.bitcast(FP8X4), rhs_scale=r_scales, start=True, stop=True,
+            )
+
+        def experts(c):
+            for g in range(GROUP):
+                cols = slice(g * C, (g + 1) * C)
+                mx(banks[c % 3][:, cols], w_codes[c % 2][:, cols], w_scales[c % 2][:, cols],
+                   x_codes[c % 2][:, cols], x_scales(c)[:, cols])
+
+        def evacuate(c):
+            for g in range(GROUP):
+                e = GROUP * c + g
+                nc.scalar.activation(
+                    out=y[:, e * C : (e + 1) * C], in_=banks[c % 3][:, g * C : (g + 1) * C],
+                    func=IDENTITY, bias=bias[:, e : e + 1],
+                )
+
+        cast_x(nc.scalar.copy, 0, 0)
+        cast_x(nc.vector.tensor_copy, 0, 1)
+        cast_x(nc.scalar.copy, 1, 0)
+        cast_x(nc.scalar.copy, 1, 1)
+        for u in range(2):
+            for c in range(2):
+                gather(u, c)
+        weave(0)
+        cast_w_chunk(0)
+        weave_shared(0)
+        cast_w_chunk(1)
+        weave_shared(1)
+        cast_w(ws_bf[:], ws_raw[:], 1)
+        for c in range(CHUNKS):
+            quantize(w_codes[c % 2], w_scales[c % 2][:], w_bf[c % 3])
+            if c + 2 < CHUNKS:
+                gather(0, c + 2)
+            elif c + 1 < CHUNKS:
+                weave(c + 1)
+            quantize(x_codes[c % 2], x_scales(c), x_bf[c])
+            if c + 2 < CHUNKS:
+                gather(1, c + 2)
+                weave(c + 1)
+            experts(c)
+            if c + 2 < CHUNKS:
+                cast_w_chunk(c + 2)
+            evacuate(c)
+
+        nc.tensor.transpose(banks[5][:, :P], gate_rows[:], ident[:])
+        nc.scalar.copy(out=gate_cols[:], in_=banks[5][:, :P])
+
+        quantize(ws_codes, ws_scales[:], ws_bf)
+        for h in range(2):
+            quantize(xs_codes[h], xs_scales[h][:], xs_bf[h])
+            for blk in range(BLOCKS):
+                cols = slice(blk * P, (blk + 1) * P)
+                mx(banks[3 + h][:, cols], xs_codes[h][:, cols], xs_scales[h][:, cols], ws_codes[:], ws_scales[:])
+            nc.scalar.copy(out=ys_t[h][:], in_=banks[3 + h][:])
+
+        def add_turned(h, src, first, last):
+            for blk in range(BLOCKS):
+                cols = slice(blk * P, (blk + 1) * P)
+                nc.tensor.matmul(
+                    sum_bank[h][:, cols], src[:, cols], ident[:], is_transpose=True,
+                    start=first and blk == 0, stop=last and blk == BLOCKS - 1,
+                )
+
+        for h in range(2):
+            add_turned(h, ys_t[h], True, False)
+
+        steps = [(h, r) for h in range(2) for r in range(TOP)]
+        for i, (h, r) in enumerate(steps):
+            window = y[:].indirect(pos_sb[r][:, h * LIST_COLS : (h + 1) * LIST_COLS])
+            if i == len(steps) - 1:
+                nc.vector.tensor_tensor(picked[i][:], window, gate_last[:], MULT)
+                nc.vector.scalar_tensor_tensor(
+                    out=result[h][:], in0=sum_bank[h][:], scalar=bias[:, E : E + 1], in1=picked[i][:], op0=ADD, op1=ADD
+                )
+                nc.sync.dma_start(out=out[:, h * HALF : (h + 1) * HALF], in_=result[h][:])
+                continue
+            nc.vector.tensor_copy(out=picked[i][:], in_=window)
+            bank = banks[(i + 5) % 6]
+            for blk in range(BLOCKS):
+                cols = slice(blk * P, (blk + 1) * P)
+                nc.tensor.transpose(bank[:, cols], picked[i][:, cols], ident[:])
+            for blk in range(BLOCKS):
+                cols = slice(blk * P, (blk + 1) * P)
+                col = 32 * r + h * BLOCKS + blk
+                nc.scalar.activation(
+                    out=scaled[i][:, cols], in_=bank[:, cols], func=COPY, scale=gate_cols[:, col : col + 1]
+                )
+            add_turned(h, scaled[i], False, r == TOP - 1 or i == len(steps) - 2)
+            if r == TOP - 1:
+                nc.scalar.activation(out=result[h][:], in_=sum_bank[h][:], func=IDENTITY, bias=bias[:, E : E + 1])
+                nc.sync.dma_start(out=out[:, h * HALF : (h + 1) * HALF], in_=result[h][:])

@@ -28,6 +28,7 @@ CHUNKS = E // GROUP
 HALF = T // 2
 BLOCKS = HALF // P
 LIST_COLS = CHUNK // 16
+SCALAR_WEAVES = (3,)
 
 
 def tile_moe_shr_lin_bias_kernel(tc, xT, w, b, gate, offs, pos1, pos2, pos3, out):
@@ -50,15 +51,21 @@ def tile_moe_shr_lin_bias_kernel(tc, xT, w, b, gate, offs, pos1, pos2, pos3, out
         def placed(name, shape, dtype, offset):
             return shared.tile(shape, dtype, name=name, align_bytes=64, offset=offset)
 
-        w_raw = [None] + [placed("w_raw%d" % c, [P, GROUP * K], F32, c * room) for c in range(1, CHUNKS)]
-        w0_raw = [placed("w0_raw%d" % i, [P, 2 * K], F32, i * room // 2) for i in range(2)]
+        side = room // 2 - 64
+
+        def start(c):
+            return c * (room + 2 * side) + side
+
+        w_raw = [None] + [placed("w_raw%d" % c, [P, GROUP * K], F32, start(c)) for c in range(1, CHUNKS)]
+        w0_raw = [placed("w0_raw%d" % i, [P, 2 * K], F32, start(0) + i * room // 2) for i in range(2)]
         ws_raw = keep.tile([P, K], F32, name="ws_raw", align_bytes=64)
         pairs = keep.tile([P, 2 * T], U32, name="pairs", align_bytes=64)
         gathered = tiles(keep, "gathered", 2, [P, 2 * CHUNK], U32)
-        gathered = gathered + [placed("gathered%d" % c, [P, 2 * CHUNK], U32, (c - 2) * room) for c in range(2, CHUNKS)]
+        gathered = gathered + [placed("gathered%d" % c, [P, 2 * CHUNK], U32, start(c - 2) - side) for c in range(2, CHUNKS)]
         x_bf = tiles(keep, "x_bf", 1, [P, PACK * CHUNK], BF16)
-        x_bf = x_bf + [placed("x_bf%d" % c, [P, PACK * CHUNK], BF16, (c - 1) * room + room // 2) for c in range(1, CHUNKS)]
-        xs_codes = [placed("xs_codes%d" % h, [P, HALF], U32, (CHUNKS - 1) * room + h * room // 4) for h in range(2)]
+        x_bf = x_bf + [placed("x_bf%d" % c, [P, PACK * CHUNK], BF16,
+                   start(c) + room // 4 if c in SCALAR_WEAVES else start(c - 1) + room - 64) for c in range(1, CHUNKS)]
+        xs_codes = [placed("xs_codes%d" % h, [P, HALF], U32, start(CHUNKS - 1) + (h == 0) * (room - 64)) for h in range(2)]
         xs_scales = tiles(keep, "xs_scales", 2, [P, HALF], U8)
         x_codes = tiles(keep, "x_codes", 2, [P, CHUNK], U32)
         last_scales = keep.tile([P, CHUNK], U8, name="last_scales", align_bytes=64)
@@ -68,12 +75,12 @@ def tile_moe_shr_lin_bias_kernel(tc, xT, w, b, gate, offs, pos1, pos2, pos3, out
         ws_bf = keep.tile([P, K], BF16, name="ws_bf", align_bytes=64)
         ws_codes = keep.tile([P, N], U32, name="ws_codes", align_bytes=64)
         ws_scales = keep.tile([P, N], U8, name="ws_scales", align_bytes=64)
-        xs_bf = tiles(keep, "xs_bf", 2, [P, PACK * HALF], BF16)
+        xs_bf = [placed("xs_bf%d" % h, [P, PACK * HALF], BF16, start(h) + room // 4) for h in range(2)]
         bias = keep.tile([P, E + 1], F32, name="bias", align_bytes=64)
         ident = keep.tile([P, P], F32, name="ident", align_bytes=64)
         gate_rows = keep.tile([P, P], F32, name="gate_rows", align_bytes=64)
         gate_cols = keep.tile([P, P], F32, name="gate_cols", align_bytes=64)
-        gate_last = keep.tile([P, HALF], F32, name="gate_last", align_bytes=64)
+        gate_last = keep.tile([P, T], F32, name="gate_last", align_bytes=64)
         y = keep.tile([P, SLOTS], F32, name="y", align_bytes=64)
         ys_t = tiles(keep, "ys_t", 2, [P, HALF], F32)
         picked = tiles(keep, "picked", 6, [P, HALF], F32)
@@ -107,25 +114,25 @@ def tile_moe_shr_lin_bias_kernel(tc, xT, w, b, gate, offs, pos1, pos2, pos3, out
 
         make_identity(nc, ident[:])
         nc.scalar.activation(out=gate_rows[:], in_=ident[:], func=IDENTITY, scale=0.0)
-        for r in range(TOP):
+        for r in range(TOP - 1):
             nc.sync.dma_start(
                 out=gate_rows[32 * r : 32 * r + T // P, :], in_=gate[r, 0, :].rearrange("(c p) -> c p", p=P)
             )
-        nc.sync.dma_start(out=gate_last[:], in_=gate[TOP - 1, :, HALF:])
+        nc.sync.dma_start(out=gate_last[:], in_=gate[TOP - 1])
         for r, pos in enumerate((pos1, pos2, pos3)):
             nc.sync.dma_start(pos_sb[r][:], pos)
 
-        def cast_x(engine_copy, u, h):
-            dst = pairs[:, u * T + h * HALF : u * T + (h + 1) * HALF].bitcast(BF16)
+        def cast_x(engine_copy, u, h, lo=0, hi=HALF):
+            dst = pairs[:, u * T + h * HALF + lo : u * T + h * HALF + hi].bitcast(BF16)
             engine_copy(
                 out=dst.rearrange("p (c i j) -> p c j i", i=4, j=2),
-                in_=x_raw[2 * u + h][:].rearrange("p j (c i) -> p c j i", i=4),
+                in_=x_raw[2 * u + h][:, :, lo:hi].rearrange("p j (c i) -> p c j i", i=4),
             )
 
         def cast_w(dst, src, count):
             nc.scalar.copy(
-                out=dst.rearrange("p (e c i j) -> p e c j i", e=count, i=4, j=PACK),
-                in_=src.rearrange("p (e j c i) -> p e c j i", e=count, i=4, j=PACK),
+                out=dst.rearrange("p (e c i j) -> p e c j i", e=count, i=2, j=PACK),
+                in_=src.rearrange("p (e j c i) -> p e c j i", e=count, i=2, j=PACK),
             )
 
         def cast_w_chunk(c):
@@ -142,15 +149,16 @@ def tile_moe_shr_lin_bias_kernel(tc, xT, w, b, gate, offs, pos1, pos2, pos3, out
             )
 
         def weave(c):
-            nc.vector.tensor_copy(
-                out=x_bf[c][:].bitcast(I32).rearrange("p (s u) -> p s u", u=2),
-                in_=gathered[c][:].bitcast(I32).rearrange("p (u s) -> p s u", u=2),
+            move, word = (nc.scalar.copy, U32) if c in SCALAR_WEAVES else (nc.vector.tensor_copy, I32)
+            move(
+                out=x_bf[c][:].bitcast(word).rearrange("p (s i u) -> p s u i", u=2, i=2),
+                in_=gathered[c][:].bitcast(word).rearrange("p (u s i) -> p s u i", u=2, i=2),
             )
 
         def weave_shared(h):
             nc.scalar.copy(
-                out=xs_bf[h][:].bitcast(U32).rearrange("p (s u) -> p s u", u=2),
-                in_=pairs[:].rearrange("p (u s) -> p s u", u=2)[:, h * HALF : (h + 1) * HALF, :],
+                out=xs_bf[h][:].bitcast(U32).rearrange("p (s i u) -> p s u i", u=2, i=2),
+                in_=pairs[:].rearrange("p (u s i) -> p s u i", u=2, i=2)[:, h * HALF // 2 : (h + 1) * HALF // 2, :, :],
             )
 
         def quantize(codes, scales, src):
@@ -182,10 +190,12 @@ def tile_moe_shr_lin_bias_kernel(tc, xT, w, b, gate, offs, pos1, pos2, pos3, out
         cast_x(nc.scalar.copy, 0, 0)
         cast_x(nc.vector.tensor_copy, 0, 1)
         cast_x(nc.scalar.copy, 1, 0)
-        cast_x(nc.scalar.copy, 1, 1)
-        for u in range(2):
-            for c in range(2):
-                gather(u, c)
+        cast_x(nc.scalar.copy, 1, 1, 0, HALF // 2)
+        for c in range(2):
+            gather(0, c)
+        cast_x(nc.vector.tensor_copy, 1, 1, HALF // 2, HALF)
+        for c in range(2):
+            gather(1, c)
         weave(0)
         cast_w_chunk(0)
         weave_shared(0)
@@ -201,10 +211,13 @@ def tile_moe_shr_lin_bias_kernel(tc, xT, w, b, gate, offs, pos1, pos2, pos3, out
             quantize(x_codes[c % 2], x_scales(c), x_bf[c])
             if c + 2 < CHUNKS:
                 gather(1, c + 2)
-                weave(c + 1)
+                if c + 1 not in SCALAR_WEAVES:
+                    weave(c + 1)
             experts(c)
             if c + 2 < CHUNKS:
                 cast_w_chunk(c + 2)
+            if c + 2 in SCALAR_WEAVES:
+                weave(c + 2)
             evacuate(c)
 
         nc.tensor.transpose(banks[5][:, :P], gate_rows[:], ident[:])
@@ -229,17 +242,11 @@ def tile_moe_shr_lin_bias_kernel(tc, xT, w, b, gate, offs, pos1, pos2, pos3, out
         for h in range(2):
             add_turned(h, ys_t[h], True, False)
 
-        steps = [(h, r) for h in range(2) for r in range(TOP)]
-        for i, (h, r) in enumerate(steps):
-            window = y[:].indirect(pos_sb[r][:, h * LIST_COLS : (h + 1) * LIST_COLS])
-            if i == len(steps) - 1:
-                nc.vector.tensor_tensor(picked[i][:], window, gate_last[:], MULT)
-                nc.vector.scalar_tensor_tensor(
-                    out=result[h][:], in0=sum_bank[h][:], scalar=bias[:, E : E + 1], in1=picked[i][:], op0=ADD, op1=ADD
-                )
-                nc.sync.dma_start(out=out[:, h * HALF : (h + 1) * HALF], in_=result[h][:])
-                continue
-            nc.vector.tensor_copy(out=picked[i][:], in_=window)
+        def window(h, r):
+            return y[:].indirect(pos_sb[r][:, h * LIST_COLS : (h + 1) * LIST_COLS])
+
+        for i, (h, r) in enumerate([(h, r) for h in range(2) for r in range(TOP - 1)]):
+            nc.vector.tensor_copy(out=picked[i][:], in_=window(h, r))
             bank = banks[(i + 5) % 6]
             for blk in range(BLOCKS):
                 cols = slice(blk * P, (blk + 1) * P)
@@ -250,7 +257,12 @@ def tile_moe_shr_lin_bias_kernel(tc, xT, w, b, gate, offs, pos1, pos2, pos3, out
                 nc.scalar.activation(
                     out=scaled[i][:, cols], in_=bank[:, cols], func=COPY, scale=gate_cols[:, col : col + 1]
                 )
-            add_turned(h, scaled[i], False, r == TOP - 1 or i == len(steps) - 2)
-            if r == TOP - 1:
-                nc.scalar.activation(out=result[h][:], in_=sum_bank[h][:], func=IDENTITY, bias=bias[:, E : E + 1])
-                nc.sync.dma_start(out=out[:, h * HALF : (h + 1) * HALF], in_=result[h][:])
+            add_turned(h, scaled[i], False, r == TOP - 2)
+        for h in range(2):
+            nc.vector.tensor_tensor(picked[4 + h][:], window(h, TOP - 1), gate_last[:, h * HALF : (h + 1) * HALF], MULT)
+        for h, lo, hi in ((0, 0, HALF), (1, 0, HALF // 2), (1, HALF // 2, HALF)):
+            nc.vector.scalar_tensor_tensor(
+                out=result[h][:, lo:hi], in0=sum_bank[h][:, lo:hi], scalar=bias[:, E : E + 1],
+                in1=picked[4 + h][:, lo:hi], op0=ADD, op1=ADD,
+            )
+            nc.sync.dma_start(out=out[:, h * HALF + lo : h * HALF + hi], in_=result[h][:, lo:hi])

@@ -28,7 +28,7 @@ CHUNKS = E // GROUP
 HALF = T // 2
 BLOCKS = HALF // P
 LIST_COLS = CHUNK // 16
-SCALAR_WEAVES = (3,)
+SCALAR_WEAVES = (0, 1, 2, 3, 4)
 
 
 def tile_moe_shr_lin_bias_kernel(tc, xT, w, b, gate, offs, pos1, pos2, pos3, out):
@@ -45,7 +45,8 @@ def tile_moe_shr_lin_bias_kernel(tc, xT, w, b, gate, offs, pos1, pos2, pos3, out
         offs_sb = lists.tile([P, SLOTS // 16], U16, name="offs_sb")
         pos_sb = [lists.tile([P, T // 16], U16, name="pos_sb%d" % r) for r in range(TOP)]
 
-        x_raw = tiles(keep, "x_raw", 4, [P, 2, HALF], F32)
+        pieces = [(0, 0, HALF), (0, HALF, HALF + HALF // 2), (0, HALF + HALF // 2, T), (1, 0, HALF), (1, HALF, T)]
+        x_raw = [keep.tile([P, 2, hi - lo], F32, name="x_raw%d" % i, align_bytes=64) for i, (u, lo, hi) in enumerate(pieces)]
         room = 4 * GROUP * K
 
         def placed(name, shape, dtype, offset):
@@ -61,21 +62,20 @@ def tile_moe_shr_lin_bias_kernel(tc, xT, w, b, gate, offs, pos1, pos2, pos3, out
         ws_raw = keep.tile([P, K], F32, name="ws_raw", align_bytes=64)
         pairs = keep.tile([P, 2 * T], U32, name="pairs", align_bytes=64)
         gathered = tiles(keep, "gathered", 2, [P, 2 * CHUNK], U32)
-        gathered = gathered + [placed("gathered%d" % c, [P, 2 * CHUNK], U32, start(c - 2) - side) for c in range(2, CHUNKS)]
-        x_bf = tiles(keep, "x_bf", 1, [P, PACK * CHUNK], BF16)
-        x_bf = x_bf + [placed("x_bf%d" % c, [P, PACK * CHUNK], BF16,
-                   start(c) + room // 4 if c in SCALAR_WEAVES else start(c - 1) + room - 64) for c in range(1, CHUNKS)]
-        xs_codes = [placed("xs_codes%d" % h, [P, HALF], U32, start(CHUNKS - 1) + (h == 0) * (room - 64)) for h in range(2)]
+        gathered = gathered + [placed("gathered%d" % c, [P, 2 * CHUNK], U32, start(c - 2) + (room - 64 if c == 2 else -side)) for c in range(2, CHUNKS)]
+        x_bf = [placed("x_bf%d" % c, [P, PACK * CHUNK], BF16,
+                   start(c) + room // 4 if c in SCALAR_WEAVES else start(c - 1) - side) for c in range(CHUNKS)]
+        xs_codes = [placed("xs_codes%d" % h, [P, HALF], U32, start(CHUNKS - 1) + h * room // 4) for h in range(2)]
         xs_scales = tiles(keep, "xs_scales", 2, [P, HALF], U8)
         x_codes = tiles(keep, "x_codes", 2, [P, CHUNK], U32)
-        last_scales = keep.tile([P, CHUNK], U8, name="last_scales", align_bytes=64)
-        w_bf = tiles(keep, "w_bf", 3, [P, GROUP * K], BF16)
+        x_scale = tiles(keep, "x_scale", 2, [P, CHUNK], U8)
+        w_bf = tiles(keep, "w_bf", 2, [P, GROUP * K], BF16)
         w_codes = tiles(keep, "w_codes", 2, [P, GROUP * N], U32)
         w_scales = tiles(keep, "w_scales", 2, [P, GROUP * N], U8)
         ws_bf = keep.tile([P, K], BF16, name="ws_bf", align_bytes=64)
         ws_codes = keep.tile([P, N], U32, name="ws_codes", align_bytes=64)
         ws_scales = keep.tile([P, N], U8, name="ws_scales", align_bytes=64)
-        xs_bf = [placed("xs_bf%d" % h, [P, PACK * HALF], BF16, start(h) + room // 4) for h in range(2)]
+        xs_bf = tiles(keep, "xs_first", 1, [P, PACK * HALF], BF16) + [placed("xs_second", [P, PACK * HALF], BF16, start(2) + room - 64)]
         bias = keep.tile([P, E + 1], F32, name="bias", align_bytes=64)
         ident = keep.tile([P, P], F32, name="ident", align_bytes=64)
         gate_rows = keep.tile([P, P], F32, name="gate_rows", align_bytes=64)
@@ -93,24 +93,26 @@ def tile_moe_shr_lin_bias_kernel(tc, xT, w, b, gate, offs, pos1, pos2, pos3, out
         x_rows = xT.rearrange("(p j) t -> p j t", j=PACK)
         w_rows = w.rearrange("e (p j) n -> p e (j n)", j=PACK)
 
-        def load_x(u, h):
-            nc.sync.dma_start(out=x_raw[2 * u + h][:], in_=x_rows[:, 2 * u : 2 * u + 2, h * HALF : (h + 1) * HALF])
+        def load_x(i):
+            u, lo, hi = pieces[i]
+            nc.sync.dma_start(out=x_raw[i][:], in_=x_rows[:, 2 * u : 2 * u + 2, lo:hi])
 
         def load_w(dst, e0, count):
             nc.sync.dma_start(out=dst[:].rearrange("p (e f) -> p e f", e=count), in_=w_rows[:, e0 : e0 + count, :])
 
-        load_x(0, 0)
-        load_x(0, 1)
+        for i in range(3):
+            load_x(i)
         nc.sync.dma_start(offs_sb[:], offs)
-        load_x(1, 0)
-        load_x(1, 1)
+        for i in range(3, 5):
+            load_x(i)
         load_w(w0_raw[0], 0, 2)
         load_w(w0_raw[1], 2, 2)
-        nc.sync.dma_start(out=bias[:], in_=b)
         load_w(w_raw[1], GROUP, GROUP)
-        load_w(ws_raw, E, 1)
+        nc.sync.dma_start(out=bias[:], in_=b)
         for c in range(2, CHUNKS):
             load_w(w_raw[c], GROUP * c, GROUP)
+            if c == 3:
+                load_w(ws_raw, E, 1)
 
         make_identity(nc, ident[:])
         nc.scalar.activation(out=gate_rows[:], in_=ident[:], func=IDENTITY, scale=0.0)
@@ -122,11 +124,12 @@ def tile_moe_shr_lin_bias_kernel(tc, xT, w, b, gate, offs, pos1, pos2, pos3, out
         for r, pos in enumerate((pos1, pos2, pos3)):
             nc.sync.dma_start(pos_sb[r][:], pos)
 
-        def cast_x(engine_copy, u, h, lo=0, hi=HALF):
-            dst = pairs[:, u * T + h * HALF + lo : u * T + h * HALF + hi].bitcast(BF16)
+        def cast_x(engine_copy, i):
+            u, lo, hi = pieces[i]
+            dst = pairs[:, u * T + lo : u * T + hi].bitcast(BF16)
             engine_copy(
                 out=dst.rearrange("p (c i j) -> p c j i", i=4, j=2),
-                in_=x_raw[2 * u + h][:, :, lo:hi].rearrange("p j (c i) -> p c j i", i=4),
+                in_=x_raw[i][:].rearrange("p j (c i) -> p c j i", i=4),
             )
 
         def cast_w(dst, src, count):
@@ -135,12 +138,19 @@ def tile_moe_shr_lin_bias_kernel(tc, xT, w, b, gate, offs, pos1, pos2, pos3, out
                 in_=src.rearrange("p (e j c i) -> p e c j i", e=count, i=2, j=PACK),
             )
 
+        def cast_w_pool(dst, src, count):
+            nc.gpsimd.tensor_scalar(
+                out=dst.rearrange("p (e n j) -> p e n j", e=count, j=PACK),
+                in0=src.rearrange("p (e j n) -> p e n j", e=count, j=PACK),
+                scalar1=1.0, scalar2=0.0, op0=MULT, op1=ADD,
+            )
+
         def cast_w_chunk(c):
-            if c == 0:
-                for s in range(2):
-                    cast_w(w_bf[0][:, s * 2 * K : (s + 1) * 2 * K], w0_raw[s][:], 2)
+            if c == 1:
+                cast_w(w_bf[1][:], w_raw[1][:], GROUP)
             else:
-                cast_w(w_bf[c % 3][:], w_raw[c][:], GROUP)
+                cast_w_pool(w_bf[c % 2][:, 2 * K :], w_raw[c][:, 2 * K :], 2)
+                cast_w(w_bf[c % 2][:, : 2 * K], w_raw[c][:, : 2 * K], 2)
 
         def gather(u, c):
             nc.vector.tensor_copy(
@@ -165,7 +175,7 @@ def tile_moe_shr_lin_bias_kernel(tc, xT, w, b, gate, offs, pos1, pos2, pos3, out
             nc.vector.quantize_mx(out=codes[:].bitcast(FP8X4), scales=scales, in_=src[:])
 
         def x_scales(c):
-            return last_scales[:] if c == CHUNKS - 1 else w_scales[c % 2][4:, :]
+            return x_scale[c % 2][:]
 
         def mx(dst, l_codes, l_scales, r_codes, r_scales):
             nc.tensor.matmul_mx(
@@ -187,38 +197,38 @@ def tile_moe_shr_lin_bias_kernel(tc, xT, w, b, gate, offs, pos1, pos2, pos3, out
                     func=IDENTITY, bias=bias[:, e : e + 1],
                 )
 
-        cast_x(nc.scalar.copy, 0, 0)
-        cast_x(nc.vector.tensor_copy, 0, 1)
-        cast_x(nc.scalar.copy, 1, 0)
-        cast_x(nc.scalar.copy, 1, 1, 0, HALF // 2)
-        for c in range(2):
-            gather(0, c)
-        cast_x(nc.vector.tensor_copy, 1, 1, HALF // 2, HALF)
-        for c in range(2):
-            gather(1, c)
-        weave(0)
-        cast_w_chunk(0)
+        cast_x(nc.scalar.copy, 0)
+        cast_x(nc.vector.tensor_copy, 1)
+        cast_x(nc.vector.tensor_copy, 2)
+        cast_x(nc.scalar.copy, 3)
+        cast_x(nc.scalar.copy, 4)
+        for u in range(2):
+            for c in range(2):
+                gather(u, c)
         weave_shared(0)
+        cast_w_pool(w_bf[0][:, : 2 * K], w0_raw[0][:], 2)
+        cast_w(w_bf[0][:, 2 * K :], w0_raw[1][:], 2)
+        weave(0)
         cast_w_chunk(1)
-        weave_shared(1)
-        cast_w(ws_bf[:], ws_raw[:], 1)
+        weave(1)
         for c in range(CHUNKS):
-            quantize(w_codes[c % 2], w_scales[c % 2][:], w_bf[c % 3])
+            quantize(w_codes[c % 2], w_scales[c % 2][:], w_bf[c % 2])
             if c + 2 < CHUNKS:
                 gather(0, c + 2)
+                gather(1, c + 2)
             elif c + 1 < CHUNKS:
                 weave(c + 1)
             quantize(x_codes[c % 2], x_scales(c), x_bf[c])
-            if c + 2 < CHUNKS:
-                gather(1, c + 2)
-                if c + 1 not in SCALAR_WEAVES:
-                    weave(c + 1)
             experts(c)
             if c + 2 < CHUNKS:
                 cast_w_chunk(c + 2)
             if c + 2 in SCALAR_WEAVES:
                 weave(c + 2)
             evacuate(c)
+            if c == 0:
+                weave_shared(1)
+            if c == 1:
+                cast_w(ws_bf[:], ws_raw[:], 1)
 
         nc.tensor.transpose(banks[5][:, :P], gate_rows[:], ident[:])
         nc.scalar.copy(out=gate_cols[:], in_=banks[5][:, :P])

@@ -10,7 +10,6 @@ FLOPS = 2 * K * N * (SLOTS + T)
 
 F32 = mybir.dt.float32
 BF16 = mybir.dt.bfloat16
-I32 = mybir.dt.int32
 U32 = mybir.dt.uint32
 U16 = mybir.dt.uint16
 U8 = mybir.dt.uint8
@@ -22,13 +21,22 @@ MULT = mybir.AluOpType.mult
 
 P = 128
 PACK = 4
+BANK = 512
 GROUP = 4
 CHUNK = GROUP * C
 CHUNKS = E // GROUP
+LAST = CHUNKS - 1
+PART = GROUP // 2
+EARLY = 3
 HALF = T // 2
+QUARTER = T // 4
 BLOCKS = HALF // P
 LIST_COLS = CHUNK // 16
-SCALAR_WEAVES = (0, 1, 2, 3, 4)
+TURNED = TOP - 1
+GATE_STEP = 32
+ROOM = 4 * GROUP * K
+
+X_PIECES = ((0, 0, HALF), (0, HALF, HALF + QUARTER), (0, HALF + QUARTER, T), (1, 0, HALF), (1, HALF, T))
 
 
 def tile_moe_shr_lin_bias_kernel(tc, xT, w, b, gate, offs, pos1, pos2, pos3, out):
@@ -36,65 +44,70 @@ def tile_moe_shr_lin_bias_kernel(tc, xT, w, b, gate, offs, pos1, pos2, pos3, out
     with ExitStack() as ctx:
         lists = ctx.enter_context(tc.tile_pool(name="lists", bufs=1))
         keep = ctx.enter_context(tc.tile_pool(name="keep", bufs=1))
-        shared = ctx.enter_context(tc.tile_pool(name="shared", bufs=1))
+        reuse = ctx.enter_context(tc.tile_pool(name="reuse", bufs=1))
         psum = ctx.enter_context(tc.psum_pool(name="psum", bufs=1))
 
-        def tiles(pool, name, count, shape, dtype):
-            return [pool.tile(shape, dtype, name="%s%d" % (name, i), align_bytes=64) for i in range(count)]
+        def tiles(name, count, shape, dtype):
+            return [keep.tile(shape, dtype, name="%s%d" % (name, i), align_bytes=64) for i in range(count)]
+
+        def placed(name, shape, dtype, offset):
+            return reuse.tile(shape, dtype, name=name, align_bytes=64, offset=offset)
+
+        def w_offset(c):
+            return (CHUNKS - EARLY) * ROOM // 2 + (c - 2) * ROOM
 
         offs_sb = lists.tile([P, SLOTS // 16], U16, name="offs_sb")
         pos_sb = [lists.tile([P, T // 16], U16, name="pos_sb%d" % r) for r in range(TOP)]
 
-        pieces = [(0, 0, HALF), (0, HALF, HALF + HALF // 2), (0, HALF + HALF // 2, T), (1, 0, HALF), (1, HALF, T)]
-        x_raw = [keep.tile([P, 2, hi - lo], F32, name="x_raw%d" % i, align_bytes=64) for i, (u, lo, hi) in enumerate(pieces)]
-        room = 4 * GROUP * K
-
-        def placed(name, shape, dtype, offset):
-            return shared.tile(shape, dtype, name=name, align_bytes=64, offset=offset)
-
-        side = room // 2 - 64
-
-        def start(c):
-            return c * (room + 2 * side) + side
-
-        w_raw = [None] + [placed("w_raw%d" % c, [P, GROUP * K], F32, start(c)) for c in range(1, CHUNKS)]
-        w0_raw = [placed("w0_raw%d" % i, [P, 2 * K], F32, start(0) + i * room // 2) for i in range(2)]
+        x_raw = [
+            keep.tile([P, 2, hi - lo], F32, name="x_raw%d" % i, align_bytes=64)
+            for i, (u, lo, hi) in enumerate(X_PIECES[:-1])
+        ]
+        w_second = keep.tile([P, GROUP * K], F32, name="w_second", align_bytes=64)
+        w_raw = {c: placed("w_raw%d" % c, [P, GROUP * K], F32, w_offset(c)) for c in range(2, CHUNKS)}
+        w_first = tiles("w_first", 2, [P, PART * K], F32)
+        x_raw.append(placed("x_raw_last", [P, 2, HALF], F32, 0))
         ws_raw = keep.tile([P, K], F32, name="ws_raw", align_bytes=64)
         pairs = keep.tile([P, 2 * T], U32, name="pairs", align_bytes=64)
-        gathered = tiles(keep, "gathered", 2, [P, 2 * CHUNK], U32)
-        gathered = gathered + [placed("gathered%d" % c, [P, 2 * CHUNK], U32, start(c - 2) + (room - 64 if c == 2 else -side)) for c in range(2, CHUNKS)]
-        x_bf = [placed("x_bf%d" % c, [P, PACK * CHUNK], BF16,
-                   start(c) + room // 4 if c in SCALAR_WEAVES else start(c - 1) - side) for c in range(CHUNKS)]
-        xs_codes = [placed("xs_codes%d" % h, [P, HALF], U32, start(CHUNKS - 1) + h * room // 4) for h in range(2)]
-        xs_scales = tiles(keep, "xs_scales", 2, [P, HALF], U8)
-        x_codes = tiles(keep, "x_codes", 2, [P, CHUNK], U32)
-        x_scale = tiles(keep, "x_scale", 2, [P, CHUNK], U8)
-        w_bf = tiles(keep, "w_bf", 2, [P, GROUP * K], BF16)
-        w_codes = tiles(keep, "w_codes", 2, [P, GROUP * N], U32)
-        w_scales = tiles(keep, "w_scales", 2, [P, GROUP * N], U8)
+        early = tiles("early", EARLY, [P, 2 * CHUNK], U32)
+        late = placed("late", [P, (CHUNKS - EARLY) * 2 * CHUNK], U32, 0)
+        gathered = [g[:] for g in early]
+        gathered = gathered + [late[:, i * 2 * CHUNK : (i + 1) * 2 * CHUNK] for i in range(CHUNKS - EARLY)]
+        x_bf = tiles("x_bf", EARLY, [P, PACK * CHUNK], BF16)
+        x_bf = x_bf + [placed("x_late%d" % c, [P, PACK * CHUNK], BF16, w_offset(c - 1)) for c in range(EARLY, CHUNKS)]
+        xs_codes = [placed("xs_codes%d" % h, [P, HALF], U32, w_offset(LAST) + h * ROOM // 4) for h in range(2)]
+        xs_scales = tiles("xs_scales", 2, [P, HALF], U8)
+        x_codes = tiles("x_codes", 2, [P, CHUNK], U32)
+        x_scales = tiles("x_scales", 2, [P, CHUNK], U8)
+        w_bf = tiles("w_bf", CHUNKS, [P, GROUP * K], BF16)
+        w_codes = tiles("w_codes", 2, [P, GROUP * N], U32)
+        w_scales = tiles("w_scales", 2, [P, GROUP * N], U8)
         ws_bf = keep.tile([P, K], BF16, name="ws_bf", align_bytes=64)
         ws_codes = keep.tile([P, N], U32, name="ws_codes", align_bytes=64)
         ws_scales = keep.tile([P, N], U8, name="ws_scales", align_bytes=64)
-        xs_bf = tiles(keep, "xs_first", 1, [P, PACK * HALF], BF16) + [placed("xs_second", [P, PACK * HALF], BF16, start(2) + room - 64)]
+        xs_bf = tiles("xs_bf", 2, [P, PACK * HALF], BF16)
         bias = keep.tile([P, E + 1], F32, name="bias", align_bytes=64)
         ident = keep.tile([P, P], F32, name="ident", align_bytes=64)
         gate_rows = keep.tile([P, P], F32, name="gate_rows", align_bytes=64)
         gate_cols = keep.tile([P, P], F32, name="gate_cols", align_bytes=64)
         gate_last = keep.tile([P, T], F32, name="gate_last", align_bytes=64)
-        y = keep.tile([P, SLOTS], F32, name="y", align_bytes=64)
-        ys_t = tiles(keep, "ys_t", 2, [P, HALF], F32)
-        picked = tiles(keep, "picked", 6, [P, HALF], F32)
-        scaled = tiles(keep, "scaled", 5, [P, HALF], F32)
-        result = tiles(keep, "result", 2, [P, HALF], F32)
+        y = placed("y", [P, SLOTS], F32, w_offset(LAST) + ROOM // 2)
+        ys_turned = tiles("ys_turned", 2, [P, HALF], F32)
+        picked = tiles("picked", 2 * TURNED, [P, HALF], F32)
+        gated = tiles("gated", 2, [P, HALF], F32)
+        scaled = tiles("scaled", 2 * TURNED, [P, HALF], F32)
+        result = tiles("result", 2, [P, HALF], F32)
 
-        banks = [psum.tile([P, 512], F32, name="bank%d" % i) for i in range(6)]
-        sum_bank = [psum.tile([P, 512], F32, name="sum_bank%d" % i) for i in range(2)]
+        banks = [psum.tile([P, BANK], F32, name="bank%d" % i) for i in range(6)]
+        y_banks = banks[:3] + banks[5:]
+        turn_banks = banks[3:5]
+        sum_banks = [psum.tile([P, BANK], F32, name="sum_bank%d" % i) for i in range(2)]
 
         x_rows = xT.rearrange("(p j) t -> p j t", j=PACK)
         w_rows = w.rearrange("e (p j) n -> p e (j n)", j=PACK)
 
         def load_x(i):
-            u, lo, hi = pieces[i]
+            u, lo, hi = X_PIECES[i]
             nc.sync.dma_start(out=x_raw[i][:], in_=x_rows[:, 2 * u : 2 * u + 2, lo:hi])
 
         def load_w(dst, e0, count):
@@ -103,176 +116,156 @@ def tile_moe_shr_lin_bias_kernel(tc, xT, w, b, gate, offs, pos1, pos2, pos3, out
         for i in range(3):
             load_x(i)
         nc.sync.dma_start(offs_sb[:], offs)
-        for i in range(3, 5):
+        for i in range(3, len(X_PIECES)):
             load_x(i)
-        load_w(w0_raw[0], 0, 2)
-        load_w(w0_raw[1], 2, 2)
-        load_w(w_raw[1], GROUP, GROUP)
+        for i in range(2):
+            load_w(w_first[i], i * PART, PART)
+        load_w(w_second, GROUP, GROUP)
         nc.sync.dma_start(out=bias[:], in_=b)
         for c in range(2, CHUNKS):
             load_w(w_raw[c], GROUP * c, GROUP)
-            if c == 3:
-                load_w(ws_raw, E, 1)
+        load_w(ws_raw, E, 1)
 
         make_identity(nc, ident[:])
         nc.scalar.activation(out=gate_rows[:], in_=ident[:], func=IDENTITY, scale=0.0)
-        for r in range(TOP - 1):
+        for r in range(TURNED):
             nc.sync.dma_start(
-                out=gate_rows[32 * r : 32 * r + T // P, :], in_=gate[r, 0, :].rearrange("(c p) -> c p", p=P)
+                out=gate_rows[GATE_STEP * r : GATE_STEP * r + T // P, :],
+                in_=gate[r, 0, :].rearrange("(c p) -> c p", p=P),
             )
         nc.sync.dma_start(out=gate_last[:], in_=gate[TOP - 1])
         for r, pos in enumerate((pos1, pos2, pos3)):
             nc.sync.dma_start(pos_sb[r][:], pos)
 
-        def cast_x(engine_copy, i):
-            u, lo, hi = pieces[i]
+        def round_x(engine_copy, i):
+            u, lo, hi = X_PIECES[i]
             dst = pairs[:, u * T + lo : u * T + hi].bitcast(BF16)
             engine_copy(
                 out=dst.rearrange("p (c i j) -> p c j i", i=4, j=2),
                 in_=x_raw[i][:].rearrange("p j (c i) -> p c j i", i=4),
             )
 
-        def cast_w(dst, src, count):
+        def round_w_scalar(dst, src, count):
             nc.scalar.copy(
                 out=dst.rearrange("p (e c i j) -> p e c j i", e=count, i=2, j=PACK),
                 in_=src.rearrange("p (e j c i) -> p e c j i", e=count, i=2, j=PACK),
             )
 
-        def cast_w_pool(dst, src, count):
+        def round_w_gpsimd(dst, src, count):
             nc.gpsimd.tensor_scalar(
                 out=dst.rearrange("p (e n j) -> p e n j", e=count, j=PACK),
                 in0=src.rearrange("p (e j n) -> p e n j", e=count, j=PACK),
                 scalar1=1.0, scalar2=0.0, op0=MULT, op1=ADD,
             )
 
-        def cast_w_chunk(c):
-            if c == 1:
-                cast_w(w_bf[1][:], w_raw[1][:], GROUP)
-            else:
-                cast_w_pool(w_bf[c % 2][:, 2 * K :], w_raw[c][:, 2 * K :], 2)
-                cast_w(w_bf[c % 2][:, : 2 * K], w_raw[c][:, : 2 * K], 2)
-
-        def gather(u, c):
+        def gather_pair(u, c):
             nc.vector.tensor_copy(
                 out=gathered[c][:, u * CHUNK : (u + 1) * CHUNK],
                 in_=pairs[:, u * T : (u + 1) * T].indirect(offs_sb[:, c * LIST_COLS : (c + 1) * LIST_COLS]),
             )
 
         def weave(c):
-            move, word = (nc.scalar.copy, U32) if c in SCALAR_WEAVES else (nc.vector.tensor_copy, I32)
-            move(
-                out=x_bf[c][:].bitcast(word).rearrange("p (s i u) -> p s u i", u=2, i=2),
-                in_=gathered[c][:].bitcast(word).rearrange("p (u s i) -> p s u i", u=2, i=2),
+            nc.scalar.copy(
+                out=x_bf[c][:].bitcast(U32).rearrange("p (s i u) -> p s u i", u=2, i=2),
+                in_=gathered[c].rearrange("p (u s i) -> p s u i", u=2, i=2),
             )
 
         def weave_shared(h):
             nc.scalar.copy(
                 out=xs_bf[h][:].bitcast(U32).rearrange("p (s i u) -> p s u i", u=2, i=2),
-                in_=pairs[:].rearrange("p (u s i) -> p s u i", u=2, i=2)[:, h * HALF // 2 : (h + 1) * HALF // 2, :, :],
+                in_=pairs[:].rearrange("p (u s i) -> p s u i", u=2, i=2)[:, h * QUARTER : (h + 1) * QUARTER, :, :],
             )
 
         def quantize(codes, scales, src):
-            nc.vector.quantize_mx(out=codes[:].bitcast(FP8X4), scales=scales, in_=src[:])
+            nc.vector.quantize_mx(out=codes[:].bitcast(FP8X4), scales=scales[:], in_=src[:])
 
-        def x_scales(c):
-            return x_scale[c % 2][:]
-
-        def mx(dst, l_codes, l_scales, r_codes, r_scales):
+        def multiply(dst, l_codes, l_scales, r_codes, r_scales):
             nc.tensor.matmul_mx(
                 out=dst, lhsT=l_codes.bitcast(FP8X4), lhsT_scale=l_scales,
                 rhs=r_codes.bitcast(FP8X4), rhs_scale=r_scales, start=True, stop=True,
             )
 
-        def experts(c):
-            for g in range(GROUP):
-                cols = slice(g * C, (g + 1) * C)
-                mx(banks[c % 3][:, cols], w_codes[c % 2][:, cols], w_scales[c % 2][:, cols],
-                   x_codes[c % 2][:, cols], x_scales(c)[:, cols])
+        def block(i):
+            return slice(i * P, (i + 1) * P)
 
-        def evacuate(c):
+        for i in range(len(X_PIECES)):
+            round_x(nc.vector.tensor_copy if i in (1, 2) else nc.scalar.copy, i)
+
+        for u in range(2):
+            for c in range(EARLY):
+                gather_pair(u, c)
+        for c in range(EARLY, CHUNKS):
+            for u in range(2):
+                gather_pair(u, c)
+
+        for i in range(2):
+            round_w_gpsimd(w_bf[0][:, i * PART * K : (i + 1) * PART * K], w_first[i][:], PART)
+        round_w_gpsimd(w_bf[1][:], w_second[:], GROUP)
+        for c in range(2, LAST):
+            round_w_gpsimd(w_bf[c][:, PART * K :], w_raw[c][:, PART * K :], PART)
+
+        for h in range(2):
+            weave_shared(h)
+        for c in range(CHUNKS):
+            if c >= EARLY:
+                round_w_scalar(w_bf[c - 1][:, : PART * K], w_raw[c - 1][:, : PART * K], PART)
+            weave(c)
+        round_w_scalar(w_bf[LAST][:], w_raw[LAST][:], GROUP)
+        round_w_scalar(ws_bf[:], ws_raw[:], 1)
+
+        for c in range(CHUNKS):
+            s = c % 2
+            bank = y_banks[c % len(y_banks)]
+            quantize(w_codes[s], w_scales[s], w_bf[c])
+            quantize(x_codes[s], x_scales[s], x_bf[c])
+            for g in range(GROUP):
+                multiply(bank[:, block(g)], w_codes[s][:, block(g)], w_scales[s][:, block(g)],
+                         x_codes[s][:, block(g)], x_scales[s][:, block(g)])
             for g in range(GROUP):
                 e = GROUP * c + g
-                nc.scalar.activation(
-                    out=y[:, e * C : (e + 1) * C], in_=banks[c % 3][:, g * C : (g + 1) * C],
-                    func=IDENTITY, bias=bias[:, e : e + 1],
-                )
+                nc.scalar.activation(out=y[:, block(e)], in_=bank[:, block(g)], func=IDENTITY, bias=bias[:, e : e + 1])
 
-        cast_x(nc.scalar.copy, 0)
-        cast_x(nc.vector.tensor_copy, 1)
-        cast_x(nc.vector.tensor_copy, 2)
-        cast_x(nc.scalar.copy, 3)
-        cast_x(nc.scalar.copy, 4)
-        for u in range(2):
-            for c in range(2):
-                gather(u, c)
-        weave_shared(0)
-        cast_w_pool(w_bf[0][:, : 2 * K], w0_raw[0][:], 2)
-        cast_w(w_bf[0][:, 2 * K :], w0_raw[1][:], 2)
-        weave(0)
-        cast_w_chunk(1)
-        weave(1)
-        for c in range(CHUNKS):
-            quantize(w_codes[c % 2], w_scales[c % 2][:], w_bf[c % 2])
-            if c + 2 < CHUNKS:
-                gather(0, c + 2)
-                gather(1, c + 2)
-            elif c + 1 < CHUNKS:
-                weave(c + 1)
-            quantize(x_codes[c % 2], x_scales(c), x_bf[c])
-            experts(c)
-            if c + 2 < CHUNKS:
-                cast_w_chunk(c + 2)
-            if c + 2 in SCALAR_WEAVES:
-                weave(c + 2)
-            evacuate(c)
-            if c == 0:
-                weave_shared(1)
-            if c == 1:
-                cast_w(ws_bf[:], ws_raw[:], 1)
+        nc.tensor.transpose(y_banks[0][:, :P], gate_rows[:], ident[:])
+        nc.scalar.copy(out=gate_cols[:], in_=y_banks[0][:, :P])
 
-        nc.tensor.transpose(banks[5][:, :P], gate_rows[:], ident[:])
-        nc.scalar.copy(out=gate_cols[:], in_=banks[5][:, :P])
-
-        quantize(ws_codes, ws_scales[:], ws_bf)
+        quantize(ws_codes, ws_scales, ws_bf)
         for h in range(2):
-            quantize(xs_codes[h], xs_scales[h][:], xs_bf[h])
-            for blk in range(BLOCKS):
-                cols = slice(blk * P, (blk + 1) * P)
-                mx(banks[3 + h][:, cols], xs_codes[h][:, cols], xs_scales[h][:, cols], ws_codes[:], ws_scales[:])
-            nc.scalar.copy(out=ys_t[h][:], in_=banks[3 + h][:])
+            quantize(xs_codes[h], xs_scales[h], xs_bf[h])
+            for i in range(BLOCKS):
+                multiply(y_banks[2 + h][:, block(i)], xs_codes[h][:, block(i)], xs_scales[h][:, block(i)],
+                         ws_codes[:], ws_scales[:])
+            nc.scalar.copy(out=ys_turned[h][:], in_=y_banks[2 + h][:])
 
-        def add_turned(h, src, first, last):
-            for blk in range(BLOCKS):
-                cols = slice(blk * P, (blk + 1) * P)
+        def add_turned_back(h, src, first, last):
+            for i in range(BLOCKS):
                 nc.tensor.matmul(
-                    sum_bank[h][:, cols], src[:, cols], ident[:], is_transpose=True,
-                    start=first and blk == 0, stop=last and blk == BLOCKS - 1,
+                    sum_banks[h][:, block(i)], src[:, block(i)], ident[:], is_transpose=True,
+                    start=first and i == 0, stop=last and i == BLOCKS - 1,
                 )
 
-        for h in range(2):
-            add_turned(h, ys_t[h], True, False)
-
-        def window(h, r):
+        def choice(h, r):
             return y[:].indirect(pos_sb[r][:, h * LIST_COLS : (h + 1) * LIST_COLS])
 
-        for i, (h, r) in enumerate([(h, r) for h in range(2) for r in range(TOP - 1)]):
-            nc.vector.tensor_copy(out=picked[i][:], in_=window(h, r))
-            bank = banks[(i + 5) % 6]
-            for blk in range(BLOCKS):
-                cols = slice(blk * P, (blk + 1) * P)
-                nc.tensor.transpose(bank[:, cols], picked[i][:, cols], ident[:])
-            for blk in range(BLOCKS):
-                cols = slice(blk * P, (blk + 1) * P)
-                col = 32 * r + h * BLOCKS + blk
-                nc.scalar.activation(
-                    out=scaled[i][:, cols], in_=bank[:, cols], func=COPY, scale=gate_cols[:, col : col + 1]
-                )
-            add_turned(h, scaled[i], False, r == TOP - 2)
         for h in range(2):
-            nc.vector.tensor_tensor(picked[4 + h][:], window(h, TOP - 1), gate_last[:, h * HALF : (h + 1) * HALF], MULT)
-        for h, lo, hi in ((0, 0, HALF), (1, 0, HALF // 2), (1, HALF // 2, HALF)):
+            add_turned_back(h, ys_turned[h], True, False)
+
+        for step, (h, r) in enumerate([(h, r) for h in range(2) for r in range(TURNED)]):
+            nc.vector.tensor_copy(out=picked[step][:], in_=choice(h, r))
+            bank = turn_banks[step % 2]
+            for i in range(BLOCKS):
+                nc.tensor.transpose(bank[:, block(i)], picked[step][:, block(i)], ident[:])
+            for i in range(BLOCKS):
+                col = GATE_STEP * r + h * BLOCKS + i
+                nc.scalar.activation(
+                    out=scaled[step][:, block(i)], in_=bank[:, block(i)], func=COPY, scale=gate_cols[:, col : col + 1]
+                )
+            add_turned_back(h, scaled[step], False, r == TURNED - 1)
+
+        for h in range(2):
+            nc.vector.tensor_tensor(gated[h][:], choice(h, TOP - 1), gate_last[:, h * HALF : (h + 1) * HALF], MULT)
+        for h, lo, hi in ((0, 0, HALF), (1, 0, QUARTER), (1, QUARTER, HALF)):
             nc.vector.scalar_tensor_tensor(
-                out=result[h][:, lo:hi], in0=sum_bank[h][:, lo:hi], scalar=bias[:, E : E + 1],
-                in1=picked[4 + h][:, lo:hi], op0=ADD, op1=ADD,
+                out=result[h][:, lo:hi], in0=sum_banks[h][:, lo:hi], scalar=bias[:, E : E + 1],
+                in1=gated[h][:, lo:hi], op0=ADD, op1=ADD,
             )
             nc.sync.dma_start(out=out[:, h * HALF + lo : h * HALF + hi], in_=result[h][:, lo:hi])

from contextlib import ExitStack

import concourse.mybir as mybir
from concourse.masks import make_identity

K, T, E, C, N = 512, 1024, 24, 128, 128
TOP = 3
SLOTS = E * C
FLOPS = 2 * K * N * (SLOTS + T)

F32 = mybir.dt.float32
BF16 = mybir.dt.bfloat16
U32 = mybir.dt.uint32
U16 = mybir.dt.uint16
U8 = mybir.dt.uint8
FP8X4 = mybir.dt.float8_e4m3fn_x4
IDENTITY = mybir.ActivationFunctionType.Identity
COPY = mybir.ActivationFunctionType.Copy
ADD = mybir.AluOpType.add
MULT = mybir.AluOpType.mult

P = 128
PACK = 4
BANK = 512
GROUP = 4
CHUNK = GROUP * C
CHUNKS = E // GROUP
LAST = CHUNKS - 1
PART = GROUP // 2
EARLY = 3
HALF = T // 2
QUARTER = T // 4
BLOCKS = HALF // P
LIST_COLS = CHUNK // 16
TURNED = TOP - 1
GATE_STEP = 32
ROOM = 4 * GROUP * K

X_PIECES = ((0, 0, HALF), (0, HALF, HALF + QUARTER), (0, HALF + QUARTER, T), (1, 0, HALF), (1, HALF, T))


def tile_moe_shr_lin_bias_kernel(tc, xT, w, b, gate, offs, pos1, pos2, pos3, out):
    nc = tc.nc
    with ExitStack() as ctx:
        lists = ctx.enter_context(tc.tile_pool(name="lists", bufs=1))
        keep = ctx.enter_context(tc.tile_pool(name="keep", bufs=1))
        reuse = ctx.enter_context(tc.tile_pool(name="reuse", bufs=1))
        psum = ctx.enter_context(tc.psum_pool(name="psum", bufs=1))

        def tiles(name, count, shape, dtype):
            return [keep.tile(shape, dtype, name="%s%d" % (name, i), align_bytes=64) for i in range(count)]

        def placed(name, shape, dtype, offset):
            return reuse.tile(shape, dtype, name=name, align_bytes=64, offset=offset)

        def w_offset(c):
            return (CHUNKS - EARLY) * ROOM // 2 + (c - 2) * ROOM

        offs_sb = lists.tile([P, SLOTS // 16], U16, name="offs_sb")
        pos_sb = [lists.tile([P, T // 16], U16, name="pos_sb%d" % r) for r in range(TOP)]

        x_raw = [
            keep.tile([P, 2, hi - lo], F32, name="x_raw%d" % i, align_bytes=64)
            for i, (u, lo, hi) in enumerate(X_PIECES[:-1])
        ]
        w_second = keep.tile([P, GROUP * K], F32, name="w_second", align_bytes=64)
        w_raw = {c: placed("w_raw%d" % c, [P, GROUP * K], F32, w_offset(c)) for c in range(2, CHUNKS)}
        w_first = tiles("w_first", 2, [P, PART * K], F32)
        x_raw.append(placed("x_raw_last", [P, 2, HALF], F32, 0))
        ws_raw = keep.tile([P, K], F32, name="ws_raw", align_bytes=64)
        pairs = keep.tile([P, 2 * T], U32, name="pairs", align_bytes=64)
        early = tiles("early", EARLY, [P, 2 * CHUNK], U32)
        late = placed("late", [P, (CHUNKS - EARLY) * 2 * CHUNK], U32, 0)
        gathered = [g[:] for g in early]
        gathered = gathered + [late[:, i * 2 * CHUNK : (i + 1) * 2 * CHUNK] for i in range(CHUNKS - EARLY)]
        x_bf = tiles("x_bf", EARLY, [P, PACK * CHUNK], BF16)
        x_bf = x_bf + [placed("x_late%d" % c, [P, PACK * CHUNK], BF16, w_offset(c - 1)) for c in range(EARLY, CHUNKS)]
        xs_codes = [placed("xs_codes%d" % h, [P, HALF], U32, w_offset(LAST) + h * ROOM // 4) for h in range(2)]
        xs_scales = tiles("xs_scales", 2, [P, HALF], U8)
        x_codes = tiles("x_codes", 2, [P, CHUNK], U32)
        x_scales = tiles("x_scales", 2, [P, CHUNK], U8)
        w_bf = tiles("w_bf", CHUNKS, [P, GROUP * K], BF16)
        w_codes = tiles("w_codes", 2, [P, GROUP * N], U32)
        w_scales = tiles("w_scales", 2, [P, GROUP * N], U8)
        ws_bf = keep.tile([P, K], BF16, name="ws_bf", align_bytes=64)
        ws_codes = keep.tile([P, N], U32, name="ws_codes", align_bytes=64)
        ws_scales = keep.tile([P, N], U8, name="ws_scales", align_bytes=64)
        xs_bf = tiles("xs_bf", 2, [P, PACK * HALF], BF16)
        bias = keep.tile([P, E + 1], F32, name="bias", align_bytes=64)
        ident = keep.tile([P, P], F32, name="ident", align_bytes=64)
        gate_rows = keep.tile([P, P], F32, name="gate_rows", align_bytes=64)
        gate_cols = keep.tile([P, P], F32, name="gate_cols", align_bytes=64)
        gate_last = keep.tile([P, T], F32, name="gate_last", align_bytes=64)
        y = placed("y", [P, SLOTS], F32, w_offset(LAST) + ROOM // 2)
        ys_turned = tiles("ys_turned", 2, [P, HALF], F32)
        picked = tiles("picked", 2 * TURNED, [P, HALF], F32)
        gated = tiles("gated", 2, [P, HALF], F32)
        scaled = tiles("scaled", 2 * TURNED, [P, HALF], F32)
        result = tiles("result", 2, [P, HALF], F32)

        banks = [psum.tile([P, BANK], F32, name="bank%d" % i) for i in range(6)]
        y_banks = banks[:3] + banks[5:]
        turn_banks = banks[3:5]
        sum_banks = [psum.tile([P, BANK], F32, name="sum_bank%d" % i) for i in range(2)]

        x_rows = xT.rearrange("(p j) t -> p j t", j=PACK)
        w_rows = w.rearrange("e (p j) n -> p e (j n)", j=PACK)

        def load_x(i):
            u, lo, hi = X_PIECES[i]
            nc.sync.dma_start(out=x_raw[i][:], in_=x_rows[:, 2 * u : 2 * u + 2, lo:hi])

        def load_w(dst, e0, count):
            nc.sync.dma_start(out=dst[:].rearrange("p (e f) -> p e f", e=count), in_=w_rows[:, e0 : e0 + count, :])

        for i in range(3):
            load_x(i)
        nc.sync.dma_start(offs_sb[:], offs)
        for i in range(3, len(X_PIECES)):
            load_x(i)
        for i in range(2):
            load_w(w_first[i], i * PART, PART)
        load_w(w_second, GROUP, GROUP)
        nc.sync.dma_start(out=bias[:], in_=b)
        for c in range(2, CHUNKS):
            load_w(w_raw[c], GROUP * c, GROUP)
        load_w(ws_raw, E, 1)

        make_identity(nc, ident[:])
        nc.scalar.activation(out=gate_rows[:], in_=ident[:], func=IDENTITY, scale=0.0)
        for r in range(TURNED):
            nc.sync.dma_start(
                out=gate_rows[GATE_STEP * r : GATE_STEP * r + T // P, :],
                in_=gate[r, 0, :].rearrange("(c p) -> c p", p=P),
            )
        nc.sync.dma_start(out=gate_last[:], in_=gate[TOP - 1])
        for r, pos in enumerate((pos1, pos2, pos3)):
            nc.sync.dma_start(pos_sb[r][:], pos)

        def round_x(engine_copy, i):
            u, lo, hi = X_PIECES[i]
            dst = pairs[:, u * T + lo : u * T + hi].bitcast(BF16)
            engine_copy(
                out=dst.rearrange("p (c i j) -> p c j i", i=4, j=2),
                in_=x_raw[i][:].rearrange("p j (c i) -> p c j i", i=4),
            )

        def round_w_scalar(dst, src, count):
            nc.scalar.copy(
                out=dst.rearrange("p (e c i j) -> p e c j i", e=count, i=2, j=PACK),
                in_=src.rearrange("p (e j c i) -> p e c j i", e=count, i=2, j=PACK),
            )

        def round_w_gpsimd(dst, src, count):
            nc.gpsimd.tensor_scalar(
                out=dst.rearrange("p (e n j) -> p e n j", e=count, j=PACK),
                in0=src.rearrange("p (e j n) -> p e n j", e=count, j=PACK),
                scalar1=1.0, scalar2=0.0, op0=MULT, op1=ADD,
            )

        def gather_pair(u, c):
            nc.vector.tensor_copy(
                out=gathered[c][:, u * CHUNK : (u + 1) * CHUNK],
                in_=pairs[:, u * T : (u + 1) * T].indirect(offs_sb[:, c * LIST_COLS : (c + 1) * LIST_COLS]),
            )

        def weave(c):
            nc.scalar.copy(
                out=x_bf[c][:].bitcast(U32).rearrange("p (s i u) -> p s u i", u=2, i=2),
                in_=gathered[c].rearrange("p (u s i) -> p s u i", u=2, i=2),
            )

        def weave_shared(h):
            nc.scalar.copy(
                out=xs_bf[h][:].bitcast(U32).rearrange("p (s i u) -> p s u i", u=2, i=2),
                in_=pairs[:].rearrange("p (u s i) -> p s u i", u=2, i=2)[:, h * QUARTER : (h + 1) * QUARTER, :, :],
            )

        def quantize(codes, scales, src):
            nc.vector.quantize_mx(out=codes[:].bitcast(FP8X4), scales=scales[:], in_=src[:])

        def multiply(dst, l_codes, l_scales, r_codes, r_scales):
            nc.tensor.matmul_mx(
                out=dst, lhsT=l_codes.bitcast(FP8X4), lhsT_scale=l_scales,
                rhs=r_codes.bitcast(FP8X4), rhs_scale=r_scales, start=True, stop=True,
            )

        def block(i):
            return slice(i * P, (i + 1) * P)

        for i in range(len(X_PIECES)):
            round_x(nc.vector.tensor_copy if i in (1, 2) else nc.scalar.copy, i)

        for u in range(2):
            for c in range(EARLY):
                gather_pair(u, c)
        for c in range(EARLY, CHUNKS):
            for u in range(2):
                gather_pair(u, c)

        for i in range(2):
            round_w_gpsimd(w_bf[0][:, i * PART * K : (i + 1) * PART * K], w_first[i][:], PART)
        round_w_gpsimd(w_bf[1][:], w_second[:], GROUP)
        for c in range(2, LAST):
            round_w_gpsimd(w_bf[c][:, PART * K :], w_raw[c][:, PART * K :], PART)

        for h in range(2):
            weave_shared(h)
        for c in range(CHUNKS):
            if c >= EARLY:
                round_w_scalar(w_bf[c - 1][:, : PART * K], w_raw[c - 1][:, : PART * K], PART)
            weave(c)
        round_w_scalar(w_bf[LAST][:], w_raw[LAST][:], GROUP)
        round_w_scalar(ws_bf[:], ws_raw[:], 1)

        for c in range(CHUNKS):
            s = c % 2
            bank = y_banks[c % len(y_banks)]
            quantize(w_codes[s], w_scales[s], w_bf[c])
            quantize(x_codes[s], x_scales[s], x_bf[c])
            for g in range(GROUP):
                multiply(bank[:, block(g)], w_codes[s][:, block(g)], w_scales[s][:, block(g)],
                         x_codes[s][:, block(g)], x_scales[s][:, block(g)])
            for g in range(GROUP):
                e = GROUP * c + g
                nc.scalar.activation(out=y[:, block(e)], in_=bank[:, block(g)], func=IDENTITY, bias=bias[:, e : e + 1])

        nc.tensor.transpose(y_banks[0][:, :P], gate_rows[:], ident[:])
        nc.scalar.copy(out=gate_cols[:], in_=y_banks[0][:, :P])

        quantize(ws_codes, ws_scales, ws_bf)
        for h in range(2):
            quantize(xs_codes[h], xs_scales[h], xs_bf[h])
            for i in range(BLOCKS):
                multiply(y_banks[2 + h][:, block(i)], xs_codes[h][:, block(i)], xs_scales[h][:, block(i)],
                         ws_codes[:], ws_scales[:])
            nc.scalar.copy(out=ys_turned[h][:], in_=y_banks[2 + h][:])

        def add_turned_back(h, src, first, last):
            for i in range(BLOCKS):
                nc.tensor.matmul(
                    sum_banks[h][:, block(i)], src[:, block(i)], ident[:], is_transpose=True,
                    start=first and i == 0, stop=last and i == BLOCKS - 1,
                )

        def choice(h, r):
            return y[:].indirect(pos_sb[r][:, h * LIST_COLS : (h + 1) * LIST_COLS])

        for h in range(2):
            add_turned_back(h, ys_turned[h], True, False)

        for step, (h, r) in enumerate([(h, r) for h in range(2) for r in range(TURNED)]):
            nc.vector.tensor_copy(out=picked[step][:], in_=choice(h, r))
            bank = turn_banks[step % 2]
            for i in range(BLOCKS):
                nc.tensor.transpose(bank[:, block(i)], picked[step][:, block(i)], ident[:])
            for i in range(BLOCKS):
                col = GATE_STEP * r + h * BLOCKS + i
                nc.scalar.activation(
                    out=scaled[step][:, block(i)], in_=bank[:, block(i)], func=COPY, scale=gate_cols[:, col : col + 1]
                )
            add_turned_back(h, scaled[step], False, r == TURNED - 1)

        for h in range(2):
            nc.vector.tensor_tensor(gated[h][:], choice(h, TOP - 1), gate_last[:, h * HALF : (h + 1) * HALF], MULT)
        for h, lo, hi in ((0, 0, HALF), (1, 0, QUARTER), (1, QUARTER, HALF)):
            nc.vector.scalar_tensor_tensor(
                out=result[h][:, lo:hi], in0=sum_banks[h][:, lo:hi], scalar=bias[:, E : E + 1],
                in1=gated[h][:, lo:hi], op0=ADD, op1=ADD,
            )
            nc.sync.dma_start(out=out[:, h * HALF + lo : h * HALF + hi], in_=result[h][:, lo:hi])
